import numpy as np
import ml_dtypes


def mxq(x, axis, fmt="e4m3"):
    dtype, down = {"e4m3": (ml_dtypes.float8_e4m3fn, 7), "e5m2": (ml_dtypes.float8_e5m2, 14)}[fmt]
    v = np.moveaxis(np.asarray(x, np.float32).astype(ml_dtypes.bfloat16).astype(np.float64), axis, -1)
    blocks = v.reshape(v.shape[:-1] + (-1, 32))
    amax = np.abs(blocks).max(-1, keepdims=True)
    byte = np.maximum(np.where(amax > 0, np.frexp(amax)[1] - 1 + 127, 0) - down, 1)
    scale = np.exp2(byte - 127.0)
    codes = (blocks / scale).astype(np.float32).astype(dtype).astype(np.float64)
    return np.moveaxis((codes * scale).reshape(v.shape), -1, axis)


WIDE = False


def mx_kscale(k):
    if not WIDE:
        return np.ones(k)
    levels = np.array([10, -10, 5, -5, 0])
    if k % 512:
        return np.exp2(np.random.permutation(np.resize(levels, k // 32))).repeat(32)
    a = np.empty((k // 512, 16))
    for p in range(k // 512):
        a[p, :8] = np.random.permutation(np.resize(levels, 8))
        for g in range(8):
            far = levels[np.abs(levels - a[p, g]) >= 10]
            a[p, g + 8] = far[np.random.randint(len(far))]
    return np.exp2(a.ravel()).repeat(32)


def f64(x):
    return np.asarray(x).astype(np.float64)


def striped(idx):
    return np.tile(idx.reshape(-1, 16).T, (8, 1)).astype(np.uint16)


def unstriped(offs):
    return offs[:16].T.reshape(-1).astype(np.int64)


def striped8(idx):
    return np.concatenate([x.reshape(-1, 16).T for x in idx]).astype(np.uint16)


def runs(offs, k):
    lists = np.stack([offs[16 * r : 16 * r + 16].T.reshape(-1) for r in range(8)]).astype(np.int64)
    return lists[np.arange(k) % 512 // 64]


def pack_weight(w):
    k, n = w.shape
    w = f64(np.asarray(w, np.float32).astype(ml_dtypes.bfloat16)).reshape(k // 32, 32, n)
    amax = np.abs(w).max(1)
    byte = np.clip(np.where(amax > 0, np.frexp(amax)[1] - 1 + 127 - 7, 1), 1, 254)
    scaled = (w * np.exp2(127.0 - byte)[:, None, :]).reshape(k, n).astype(np.float32)
    words = np.ascontiguousarray(scaled.reshape(k // 512, 128, 4, n).transpose(0, 1, 3, 2)).astype(ml_dtypes.float8_e4m3fn).view(np.uint8)
    return words, np.ascontiguousarray(byte.astype(np.uint8).reshape(k // 512, 16, n))


def unpack_weight(words, scales):
    g, p, n, _ = words.shape
    vals = np.ascontiguousarray(words).view(ml_dtypes.float8_e4m3fn).astype(np.float64) * np.repeat(np.exp2(scales.astype(np.float64) - 127.0), 8, axis=1)[..., None]
    return vals.transpose(0, 1, 3, 2).reshape(g * 512, n)


def sigmoid(v):
    return 1.0 / (1.0 + np.exp(-np.maximum(v, -700.0)))


K, T, S, H, W, G = 512, 1024, 256, 512, 128, 2048


def setup_inputs():
    n = np.random.standard_normal
    s = mx_kscale(K)[:, None]
    packed_xT = pack_weight(n((K, T)) * s)
    packed_dT = pack_weight(n((K, G)) / s)
    perm = np.random.permutation(S)
    return {
        "x_words": packed_xT[0],
        "x_scales": packed_xT[1],
        "w1": (n((K, H)) / np.sqrt(K) / s).astype(np.float32),
        "gs": (np.random.uniform(0.5, 1.5, (K, 1)) * s).astype(np.float32),
        "d_words": packed_dT[0],
        "d_scales": packed_dT[1],
        "sl": np.random.uniform(1.0, 2.0, (H, 1)).astype(np.float32),
        "th": (0.5 * n((H, 1))).astype(np.float32),
        "offs": striped(np.random.permutation(T)[:S]),
        "n1": striped(perm[:W]),
        "n2": striped(perm[W:]),
        "n3": striped(np.random.permutation(S)),
        "k1": striped8(np.random.randint(0, G, (8, H))),
        "k2": striped8(np.random.randint(0, G, (8, H))),
        "two": striped(np.random.permutation(T)[:S]),
        "n4": striped8(np.stack([np.random.permutation(S) for _ in range(8)])),
        "n5": striped8(np.stack([np.random.permutation(S) for _ in range(8)])),
    }


def reference(x_words, x_scales, w1, gs, d_words, d_scales, sl, th, offs, n1, n2, n3, k1, k2, two, n4, n5):
    d_k1 = unpack_weight(d_words, d_scales)[np.arange(K)[:, None], runs(k1, K)]
    xq = unpack_weight(x_words, x_scales)[:, unstriped(offs)]
    y = mxq(f64(w1), 0, "e4m3").T @ xq
    pa = y[:, unstriped(n1)]
    pb = y[:, unstriped(n2)]
    rb = pa - pb
    ra = pa + pb
    ds = np.zeros((H, S))
    ds[:, unstriped(n1)] = ra
    dt = ds.copy()
    dt[:, unstriped(n2)] = rb
    z = f64(gs) * (np.maximum(dt, dt[:, unstriped(n3)]))
    d_k2 = unpack_weight(d_words, d_scales)[np.arange(K)[:, None], runs(k2, K)]
    x_two = unpack_weight(x_words, x_scales)[:, unstriped(two)]
    h = 0.0625 * ((d_k1.T @ mxq(z, 0, "e4m3") + d_k2.T @ x_two))
    st = h - (h[np.arange(H)[:, None], runs(n4, H)])
    sg = sigmoid(f64(sl) * (st[np.arange(H)[:, None], runs(n5, H)] - f64(th)))
    return h * sg

@@ -1,0 +1,237 @@
+from contextlib import ExitStack
+
+import concourse.mybir as mybir
+
+F32 = mybir.dt.float32
+BF16 = mybir.dt.bfloat16
+I32 = mybir.dt.int32
+U32 = mybir.dt.uint32
+U16 = mybir.dt.uint16
+U8 = mybir.dt.uint8
+FP8X4 = mybir.dt.float8_e4m3fn_x4
+ALU = mybir.AluOpType
+ACT = mybir.ActivationFunctionType
+
+K, T, S, H, W, G = 512, 1024, 256, 512, 128, 2048
+P = 128
+PACK = 4
+HALF = S // 2
+SPARE = 8
+WHOLE = 2
+FLOPS = 3 * 2 * K * H * S
+
+
+def tile_picked_cmixhaarhehq_none_p_kernel(
+    tc, x_words, x_scales, w1, gs, d_words, d_scales, sl, th, offs, n1, n2, n3, k1, k2, two, n4, n5, out
+):
+    nc = tc.nc
+    with ExitStack() as ctx:
+        keep = ctx.enter_context(tc.tile_pool(name="keep", bufs=1))
+        psum = ctx.enter_context(tc.psum_pool(name="psum", bufs=1))
+
+        def sb(name, shape, dtype, tag=""):
+            return keep.tile(shape, dtype, name=name, tag=tag or name, align_bytes=64)
+
+        def load_list(name, src):
+            tile = sb(name, list(src.shape), U16)
+            nc.sync.dma_start(tile[:], src)
+            return tile
+
+        x_byte_table = sb("x_byte_table", [P, T], U8)
+        d_byte_table = sb("d_byte_table", [P, G], U8)
+        d_planes = sb("d_planes", [P, 2, H], U8)
+        nc.vector.memset(x_byte_table[:].bitcast(I32), 0)
+        nc.gpsimd.memset(d_byte_table[:].bitcast(I32), 0)
+        nc.vector.memset(d_planes[:].rearrange("p l c -> p (l c)").bitcast(I32), 0)
+
+        nc.gpsimd.dma_start(d_byte_table[0:P:8, :].bitcast(I32), d_scales[0].bitcast(I32))
+        w_rows = w1.rearrange("(p j) c -> p j c", j=PACK)
+        w_raw = [sb("w_raw%d" % c, [P, PACK, H // 2], F32) for c in range(2)]
+        nc.sync.dma_start(w_raw[0][:], w_rows[:, :, 0 : H // 2])
+        for r in range(4):
+            nc.sync.dma_start(x_byte_table[r:P:32, :].bitcast(I32), x_scales[0, r:16:4, :].bitcast(I32))
+        offs_t = load_list("offs_t", offs)
+        nc.sync.dma_start(w_raw[1][:], w_rows[:, :, H // 2 : H])
+        x_word_table = sb("x_word_table", [P, T], U32)
+        nc.sync.dma_start(x_word_table[:].bitcast(I32), x_words[0].rearrange("p n t -> p (n t)").bitcast(I32))
+        d_word_table = sb("d_word_table", [P, G], U32)
+        nc.sync.dma_start(d_word_table[:].bitcast(I32), d_words[0].rearrange("p n t -> p (n t)").bitcast(I32))
+        n1_t = load_list("n1_t", n1)
+        n2_t = load_list("n2_t", n2)
+        two_t = load_list("two_t", two)
+        k1_t = load_list("k1_t", k1)
+        k2_t = load_list("k2_t", k2)
+        n3_t = load_list("n3_t", n3)
+        n4_t = load_list("n4_t", n4)
+        n5_t = load_list("n5_t", n5)
+
+        gs_t = sb("gs_t", [P, PACK], F32)
+        sl_t = sb("sl_t", [P, PACK], F32)
+        th_t = sb("th_t", [P, PACK], F32)
+        for tile, src in ((gs_t, gs), (sl_t, sl), (th_t, th)):
+            nc.sync.dma_start(tile[:], src.rearrange("(p t) o -> p (t o)", t=PACK))
+
+        w_pairs = [sb("w_pairs%d" % u, [P, 2, P, PACK], BF16) for u in range(2)]
+        xq_bytes = sb("xq_bytes", [P, S], U8)
+        nc.vector.tensor_copy(xq_bytes[:], x_byte_table[:].indirect(offs_t[:]))
+        for c in range(2):
+            src = w_raw[c][:].rearrange("p j (m t) -> p m j t", t=PACK)
+            cols = slice(64 * c, 64 * c + 64)
+            nc.vector.tensor_copy(w_pairs[0][:, :, cols, :].rearrange("p t m j -> p m j t"), src[:, :, :, 0:2])
+            nc.scalar.copy(w_pairs[1][:, :, cols, :].rearrange("p t m j -> p m j t"), src[:, :, :, 2:4])
+        w_codes = [sb("w_codes%d" % t, [P, P], U32) for t in range(PACK)]
+        w_planes = [sb("w_planes%d" % t, [P, P], U8) for t in range(PACK)]
+
+        def quantise_w(t):
+            nc.vector.quantize_mx(
+                out=w_codes[t][:].bitcast(FP8X4),
+                scales=w_planes[t][:],
+                in_=w_pairs[t // 2][:, t % 2, :, :].rearrange("p m j -> p (m j)"),
+            )
+
+        quantise_w(0)
+        quantise_w(1)
+        xq_words = sb("xq_words", [P, S], U32)
+        nc.vector.tensor_copy(xq_words[:], x_word_table[:].indirect(offs_t[:]))
+        quantise_w(2)
+        quantise_w(3)
+
+        y = [sb("y%d" % t, [P, S], F32) for t in range(PACK)]
+        pa = [sb("pa%d" % t, [P, W], F32) for t in range(PACK)]
+        pb = [sb("pb%d" % t, [P, W], F32) for t in range(PACK)]
+        ra = [sb("ra%d" % t, [P, W], F32) for t in range(PACK)]
+        rb = [sb("rb%d" % t, [P, W], F32) for t in range(PACK)]
+        dt = [sb("dt%d" % t, [P, S + SPARE], F32) for t in range(PACK)]
+        for t in range(PACK):
+            nc.gpsimd.memset(dt[t][:, S : S + SPARE], 0.0)
+        partner = [sb("partner%d" % t, [P, S], F32) for t in range(PACK)]
+        for t in range(PACK):
+            acc = psum.tile([P, S], F32, name="acc_y%d" % t, tag="bank%d" % t)
+            nc.tensor.matmul_mx(
+                out=acc[:],
+                lhsT=w_codes[t][:].bitcast(FP8X4),
+                lhsT_scale=w_planes[t][:],
+                rhs=xq_words[:].bitcast(FP8X4),
+                rhs_scale=xq_bytes[:],
+                start=True,
+                stop=True,
+            )
+            if t == 0:
+                nc.scalar.copy(y[t][:], acc[:])
+            else:
+                nc.vector.tensor_copy(y[t][:], acc[:])
+        for t in range(PACK):
+            nc.scalar.activation(pa[t][:], y[t][:].indirect(n1_t[:]), ACT.Copy)
+            nc.scalar.activation(pb[t][:], y[t][:].indirect(n2_t[:]), ACT.Copy)
+            nc.vector.tensor_tensor(ra[t][:], pa[t][:], pb[t][:], ALU.add)
+            nc.vector.tensor_tensor(rb[t][:], pa[t][:], pb[t][:], ALU.subtract)
+        for t in range(PACK):
+            nc.scalar.activation(dt[t][:].indirect(n1_t[:]), ra[t][:], ACT.Copy)
+            nc.scalar.activation(dt[t][:].indirect(n2_t[:]), rb[t][:], ACT.Copy)
+            width = S if t < WHOLE else HALF
+            nc.scalar.activation(partner[t][:, 0:width], dt[t][:].indirect(n3_t[:, 0 : width // 16]), ACT.Copy)
+        for t in range(WHOLE, PACK):
+            nc.scalar.activation(partner[t][:, HALF:S], dt[t][:].indirect(n3_t[:, HALF // 16 : S // 16]), ACT.Copy)
+
+        d_bytes_dealt = sb("d_bytes_dealt", [P, 2, H], U8)
+        for l, lists in enumerate((k1_t, k2_t)):
+            d_bytes = sb("d_bytes%d" % l, [P, H], U8, tag="pb%d" % l)
+            nc.vector.tensor_copy(d_bytes[:], d_byte_table[:].indirect(lists[:]))
+            nc.vector.tensor_copy(
+                d_bytes_dealt[:, l, :].rearrange("p (t m) -> p m t", t=PACK),
+                d_bytes[:].rearrange("p (m t) -> p m t", t=PACK),
+            )
+        for r in range(4):
+            nc.sync.dma_start(
+                d_planes[r:P:32].rearrange("p l c -> p (l c)").bitcast(I32),
+                d_bytes_dealt[8 * r : P : 32].rearrange("p l c -> p (l c)").bitcast(I32),
+            )
+        x2_bytes = sb("x2_bytes", [P, S], U8)
+        x2_words = sb("x2_words", [P, S], U32)
+        nc.vector.tensor_copy(x2_bytes[:], x_byte_table[:].indirect(two_t[:]))
+        nc.vector.tensor_copy(x2_words[:], x_word_table[:].indirect(two_t[:]))
+        d_codes = [None, None]
+        for l, lists in ((1, k2_t), (0, k1_t)):
+            picked = sb("d_picked%d" % l, [P, H], U32, tag="pa%d" % (1 - l))
+            nc.vector.tensor_copy(picked[:], d_word_table[:].indirect(lists[:]))
+            d_codes[l] = sb("d_codes%d" % l, [P, H], U32)
+            nc.vector.tensor_copy(
+                d_codes[l][:].rearrange("p (t m) -> p m t", t=PACK),
+                picked[:].rearrange("p (m t) -> p m t", t=PACK),
+            )
+        bias_t = sb("bias_t", [P, PACK], F32)
+        nc.vector.scalar_tensor_tensor(bias_t[:], sl_t[:], -1.0, th_t[:], ALU.mult, ALU.mult)
+
+        h = [sb("h%d" % t, [P, 2 * S], F32) for t in range(PACK)]
+        st = [sb("st%d" % t, [P, 2 * S], F32) for t in range(PACK)]
+        for t in range(PACK):
+            nc.gpsimd.memset(h[t][:, S : 2 * S], 0.0)
+            nc.gpsimd.memset(st[t][:, S : 2 * S], 0.0)
+        larger = sb("larger", [P, PACK, S], F32)
+        for t in range(WHOLE):
+            nc.vector.tensor_tensor(larger[:, t, :], dt[t][:, 0:S], partner[t][:], ALU.max)
+        z = sb("z", [P, S, PACK], BF16)
+
+        def weigh(t0, cols):
+            groups = (cols.stop - cols.start) // 4
+            nc.vector.tensor_tensor(
+                z[:, cols, t0 : t0 + 2].rearrange("p (c i) t -> p c t i", i=4),
+                larger[:, t0 : t0 + 2, cols].rearrange("p t (c i) -> p c t i", i=4),
+                gs_t[:, t0 : t0 + 2].unsqueeze(1).unsqueeze(3).to_broadcast([P, groups, 2, 4]),
+                ALU.mult,
+            )
+
+        weigh(0, slice(0, S))
+        for c in range(2):
+            cols = slice(HALF * c, HALF * (c + 1))
+            acc_h = [psum.tile([P, HALF], F32, name="acc_h%d_%d" % (c, t), tag="bank%d" % (4 * (1 - c) + t)) for t in range(PACK)]
+            for t in range(PACK):
+                rows = slice(P * t, P * (t + 1))
+                nc.tensor.matmul_mx(
+                    out=acc_h[t][:],
+                    lhsT=d_codes[1][:, rows].bitcast(FP8X4),
+                    lhsT_scale=d_planes[:, 1, rows],
+                    rhs=x2_words[:, cols].bitcast(FP8X4),
+                    rhs_scale=x2_bytes[:, cols],
+                    start=True,
+                    stop=False,
+                )
+            for t in range(WHOLE, PACK):
+                nc.vector.tensor_tensor(larger[:, t, cols], dt[t][:, cols], partner[t][:, cols], ALU.max)
+            weigh(2, cols)
+            z_codes = sb("z_codes%d" % c, [P, HALF], U32)
+            z_plane = sb("z_plane%d" % c, [P, HALF], U8)
+            nc.vector.quantize_mx(out=z_codes[:].bitcast(FP8X4), scales=z_plane[:], in_=z[:, cols, :].rearrange("p j t -> p (j t)"))
+            for t in range(PACK):
+                rows = slice(P * t, P * (t + 1))
+                nc.tensor.matmul_mx(
+                    out=acc_h[t][:],
+                    lhsT=d_codes[0][:, rows].bitcast(FP8X4),
+                    lhsT_scale=d_planes[:, 0, rows],
+                    rhs=z_codes[:].bitcast(FP8X4),
+                    rhs_scale=z_plane[:],
+                    start=False,
+                    stop=True,
+                )
+                if c == 0:
+                    nc.scalar.activation(h[t][:, cols], acc_h[t][:], ACT.Copy, scale=0.0625)
+                else:
+                    nc.vector.tensor_scalar(h[t][:, cols], acc_h[t][:], 0.0625, None, ALU.mult)
+
+        out_rows = out.rearrange("(p t) j -> p t j", t=PACK)
+        for t in range(PACK):
+            other = sb("other%d" % t, [P, S], F32)
+            nc.scalar.activation(other[:], h[t][:].indirect(n4_t[:]), ACT.Copy)
+            nc.vector.tensor_tensor(st[t][:, 0:S], h[t][:, 0:S], other[:], ALU.subtract)
+        for t in range(PACK):
+            sg = sb("sg%d" % t, [P, S], F32)
+            res = sb("res%d" % t, [P, S], F32)
+            nc.scalar.activation(
+                sg[:],
+                st[t][:].indirect(n5_t[:]),
+                ACT.Sigmoid,
+                bias=bias_t[:, t : t + 1],
+                scale=sl_t[:, t : t + 1],
+            )
+            nc.vector.tensor_tensor(res[:], h[t][:, 0:S], sg[:], ALU.mult)
+            nc.sync.dma_start(out_rows[:, t, :], res[:])

@@ -44,6 +44,11 @@ def tile_picked_cmixhaarhehq_none_p_kernel(
         nc.gpsimd.memset(d_byte_table[:].bitcast(I32), 0)
         nc.vector.memset(d_planes[:].rearrange("p l c -> p (l c)").bitcast(I32), 0)
 
+        warm_in = sb("warm_in", [P, 1], F32)
+        warm_out = sb("warm_out", [P, 1], F32)
+        nc.vector.memset(warm_in[:], 0.0)
+        nc.scalar.activation(warm_out[:], warm_in[:], ACT.Sigmoid)
+
         nc.gpsimd.dma_start(d_byte_table[0:P:8, :].bitcast(I32), d_scales[0].bitcast(I32))
         w_rows = w1.rearrange("(p j) c -> p j c", j=PACK)
         w_raw = [sb("w_raw%d" % c, [P, PACK, H // 2], F32) for c in range(2)]

@@ -17,7 +17,8 @@ P = 128
 PACK = 4
 HALF = S // 2
 SPARE = 8
-WHOLE = 2
+EARLY = 2
+W_SPLIT = 80
 FLOPS = 3 * 2 * K * H * S
 
 
@@ -37,35 +38,38 @@ def tile_picked_cmixhaarhehq_none_p_kernel(
             nc.sync.dma_start(tile[:], src)
             return tile
 
+        def entries(lists, cols):
+            return lists[:, cols.start // 16 : cols.stop // 16]
+
         x_byte_table = sb("x_byte_table", [P, T], U8)
         d_byte_table = sb("d_byte_table", [P, G], U8)
-        d_planes = sb("d_planes", [P, 2, H], U8)
+        d_moved = sb("d_moved", [P, H], U8)
         nc.vector.memset(x_byte_table[:].bitcast(I32), 0)
-        nc.gpsimd.memset(d_byte_table[:].bitcast(I32), 0)
-        nc.vector.memset(d_planes[:].rearrange("p l c -> p (l c)").bitcast(I32), 0)
+        nc.vector.memset(d_byte_table[:].bitcast(I32), 0)
+        nc.vector.memset(d_moved[:].bitcast(I32), 0)
 
         warm_in = sb("warm_in", [P, 1], F32)
         warm_out = sb("warm_out", [P, 1], F32)
         nc.vector.memset(warm_in[:], 0.0)
         nc.scalar.activation(warm_out[:], warm_in[:], ACT.Sigmoid)
 
-        nc.gpsimd.dma_start(d_byte_table[0:P:8, :].bitcast(I32), d_scales[0].bitcast(I32))
         w_rows = w1.rearrange("(p j) c -> p j c", j=PACK)
-        w_raw = [sb("w_raw%d" % c, [P, PACK, H // 2], F32) for c in range(2)]
-        nc.sync.dma_start(w_raw[0][:], w_rows[:, :, 0 : H // 2])
+        w_raw = sb("w_raw", [P, PACK, H], F32)
+        nc.sync.dma_start(w_raw[:, 0:2, :], w_rows[:, 0:2, :])
         for r in range(4):
             nc.sync.dma_start(x_byte_table[r:P:32, :].bitcast(I32), x_scales[0, r:16:4, :].bitcast(I32))
         offs_t = load_list("offs_t", offs)
-        nc.sync.dma_start(w_raw[1][:], w_rows[:, :, H // 2 : H])
+        nc.sync.dma_start(w_raw[:, 2:4, :], w_rows[:, 2:4, :])
         x_word_table = sb("x_word_table", [P, T], U32)
         nc.sync.dma_start(x_word_table[:].bitcast(I32), x_words[0].rearrange("p n t -> p (n t)").bitcast(I32))
-        d_word_table = sb("d_word_table", [P, G], U32)
-        nc.sync.dma_start(d_word_table[:].bitcast(I32), d_words[0].rearrange("p n t -> p (n t)").bitcast(I32))
         n1_t = load_list("n1_t", n1)
         n2_t = load_list("n2_t", n2)
         two_t = load_list("two_t", two)
         k1_t = load_list("k1_t", k1)
+        nc.sync.dma_start(d_byte_table[0:P:8, :].bitcast(I32), d_scales[0].bitcast(I32))
         k2_t = load_list("k2_t", k2)
+        d_word_table = sb("d_word_table", [P, G], U32)
+        nc.sync.dma_start(d_word_table[:].bitcast(I32), d_words[0].rearrange("p n t -> p (n t)").bitcast(I32))
         n3_t = load_list("n3_t", n3)
         n4_t = load_list("n4_t", n4)
         n5_t = load_list("n5_t", n5)
@@ -79,101 +83,98 @@ def tile_picked_cmixhaarhehq_none_p_kernel(
         w_pairs = [sb("w_pairs%d" % u, [P, 2, P, PACK], BF16) for u in range(2)]
         xq_bytes = sb("xq_bytes", [P, S], U8)
         nc.vector.tensor_copy(xq_bytes[:], x_byte_table[:].indirect(offs_t[:]))
-        for c in range(2):
-            src = w_raw[c][:].rearrange("p j (m t) -> p m j t", t=PACK)
-            cols = slice(64 * c, 64 * c + 64)
-            nc.vector.tensor_copy(w_pairs[0][:, :, cols, :].rearrange("p t m j -> p m j t"), src[:, :, :, 0:2])
-            nc.scalar.copy(w_pairs[1][:, :, cols, :].rearrange("p t m j -> p m j t"), src[:, :, :, 2:4])
+        w_src = w_raw[:].rearrange("p j (m t) -> p m j t", t=PACK)
+        w_dst = [w_pairs[u][:].rearrange("p t m j -> p m j t") for u in range(2)]
+        nc.vector.tensor_copy(w_dst[0][:, 0:W_SPLIT], w_src[:, 0:W_SPLIT, :, 0:2])
+        nc.scalar.copy(w_dst[0][:, W_SPLIT:P], w_src[:, W_SPLIT:P, :, 0:2])
+        nc.scalar.copy(w_dst[1], w_src[:, :, :, 2:4])
         w_codes = [sb("w_codes%d" % t, [P, P], U32) for t in range(PACK)]
-        w_planes = [sb("w_planes%d" % t, [P, P], U8) for t in range(PACK)]
+        w_scales = [sb("w_scales%d" % t, [P, P], U8) for t in range(PACK)]
 
         def quantise_w(t):
             nc.vector.quantize_mx(
                 out=w_codes[t][:].bitcast(FP8X4),
-                scales=w_planes[t][:],
+                scales=w_scales[t][:],
                 in_=w_pairs[t // 2][:, t % 2, :, :].rearrange("p m j -> p (m j)"),
             )
 
         quantise_w(0)
-        quantise_w(1)
         xq_words = sb("xq_words", [P, S], U32)
         nc.vector.tensor_copy(xq_words[:], x_word_table[:].indirect(offs_t[:]))
-        quantise_w(2)
-        quantise_w(3)
+        for t in range(1, PACK):
+            quantise_w(t)
 
         y = [sb("y%d" % t, [P, S], F32) for t in range(PACK)]
-        pa = [sb("pa%d" % t, [P, W], F32) for t in range(PACK)]
-        pb = [sb("pb%d" % t, [P, W], F32) for t in range(PACK)]
-        ra = [sb("ra%d" % t, [P, W], F32) for t in range(PACK)]
-        rb = [sb("rb%d" % t, [P, W], F32) for t in range(PACK)]
+        pa = [sb("pa%d" % u, [P, 2, W], F32) for u in range(2)]
+        pb = [sb("pb%d" % u, [P, 2, W], F32) for u in range(2)]
+        ra = [sb("ra%d" % u, [P, 2, W], F32) for u in range(2)]
+        rb = [sb("rb%d" % u, [P, 2, W], F32) for u in range(2)]
         dt = [sb("dt%d" % t, [P, S + SPARE], F32) for t in range(PACK)]
-        for t in range(PACK):
-            nc.gpsimd.memset(dt[t][:, S : S + SPARE], 0.0)
         partner = [sb("partner%d" % t, [P, S], F32) for t in range(PACK)]
         for t in range(PACK):
-            acc = psum.tile([P, S], F32, name="acc_y%d" % t, tag="bank%d" % t)
+            acc_y = psum.tile([P, S], F32, name="acc_y%d" % t, tag="bank%d" % t)
             nc.tensor.matmul_mx(
-                out=acc[:],
+                out=acc_y[:],
                 lhsT=w_codes[t][:].bitcast(FP8X4),
-                lhsT_scale=w_planes[t][:],
+                lhsT_scale=w_scales[t][:],
                 rhs=xq_words[:].bitcast(FP8X4),
                 rhs_scale=xq_bytes[:],
                 start=True,
                 stop=True,
             )
             if t == 0:
-                nc.scalar.copy(y[t][:], acc[:])
+                nc.scalar.copy(y[t][:], acc_y[:])
             else:
-                nc.vector.tensor_copy(y[t][:], acc[:])
+                nc.vector.tensor_copy(y[t][:], acc_y[:])
         for t in range(PACK):
-            nc.scalar.activation(pa[t][:], y[t][:].indirect(n1_t[:]), ACT.Copy)
-            nc.scalar.activation(pb[t][:], y[t][:].indirect(n2_t[:]), ACT.Copy)
-            nc.vector.tensor_tensor(ra[t][:], pa[t][:], pb[t][:], ALU.add)
-            nc.vector.tensor_tensor(rb[t][:], pa[t][:], pb[t][:], ALU.subtract)
-        for t in range(PACK):
-            nc.scalar.activation(dt[t][:].indirect(n1_t[:]), ra[t][:], ACT.Copy)
-            nc.scalar.activation(dt[t][:].indirect(n2_t[:]), rb[t][:], ACT.Copy)
-            width = S if t < WHOLE else HALF
-            nc.scalar.activation(partner[t][:, 0:width], dt[t][:].indirect(n3_t[:, 0 : width // 16]), ACT.Copy)
-        for t in range(WHOLE, PACK):
-            nc.scalar.activation(partner[t][:, HALF:S], dt[t][:].indirect(n3_t[:, HALF // 16 : S // 16]), ACT.Copy)
+            nc.scalar.activation(pa[t // 2][:, t % 2, :], y[t][:].indirect(n1_t[:]), ACT.Copy)
+            nc.scalar.activation(pb[t // 2][:, t % 2, :], y[t][:].indirect(n2_t[:]), ACT.Copy)
+            if t % 2 == 1:
+                nc.vector.tensor_tensor(ra[t // 2][:], pa[t // 2][:], pb[t // 2][:], ALU.add)
+                nc.vector.tensor_tensor(rb[t // 2][:], pa[t // 2][:], pb[t // 2][:], ALU.subtract)
+        for u in range(2):
+            for lists, values in ((n1_t, ra[u]), (n2_t, rb[u])):
+                for e in range(2):
+                    nc.scalar.activation(dt[2 * u + e][:].indirect(lists[:]), values[:, e, :], ACT.Copy)
+            for t in (2 * u, 2 * u + 1):
+                cols = slice(0, S if t < EARLY else HALF)
+                nc.scalar.activation(partner[t][:, cols], dt[t][:].indirect(entries(n3_t, cols)), ACT.Copy)
+        for t in range(EARLY, PACK):
+            cols = slice(HALF, S)
+            nc.scalar.activation(partner[t][:, cols], dt[t][:].indirect(entries(n3_t, cols)), ACT.Copy)
 
-        d_bytes_dealt = sb("d_bytes_dealt", [P, 2, H], U8)
         for l, lists in enumerate((k1_t, k2_t)):
-            d_bytes = sb("d_bytes%d" % l, [P, H], U8, tag="pb%d" % l)
+            d_bytes = sb("d_bytes%d" % l, [P, H], U8, tag="w_codes%d" % (PACK - 1 - l))
             nc.vector.tensor_copy(d_bytes[:], d_byte_table[:].indirect(lists[:]))
-            nc.vector.tensor_copy(
-                d_bytes_dealt[:, l, :].rearrange("p (t m) -> p m t", t=PACK),
-                d_bytes[:].rearrange("p (m t) -> p m t", t=PACK),
-            )
-        for r in range(4):
-            nc.sync.dma_start(
-                d_planes[r:P:32].rearrange("p l c -> p (l c)").bitcast(I32),
-                d_bytes_dealt[8 * r : P : 32].rearrange("p l c -> p (l c)").bitcast(I32),
-            )
-        x2_bytes = sb("x2_bytes", [P, S], U8)
-        x2_words = sb("x2_words", [P, S], U32)
+            for r in range(4):
+                nc.sync.dma_start(d_moved[4 * l + r : P : 32, :].bitcast(I32), d_bytes[8 * r : P : 32, :].bitcast(I32))
+        x2_bytes = sb("x2_bytes", [P, S], U8, tag="w_scales%d" % (PACK - 1))
         nc.vector.tensor_copy(x2_bytes[:], x_byte_table[:].indirect(two_t[:]))
+        x2_words = sb("x2_words", [P, S], U32)
         nc.vector.tensor_copy(x2_words[:], x_word_table[:].indirect(two_t[:]))
-        d_codes = [None, None]
+        picked = [None, None]
         for l, lists in ((1, k2_t), (0, k1_t)):
-            picked = sb("d_picked%d" % l, [P, H], U32, tag="pa%d" % (1 - l))
-            nc.vector.tensor_copy(picked[:], d_word_table[:].indirect(lists[:]))
+            picked[l] = sb("d_picked%d" % l, [P, H], U32, tag=("pa0", "pb0")[l])
+            nc.vector.tensor_copy(picked[l][:], d_word_table[:].indirect(lists[:]))
+        d_codes = [None, None]
+        for l in (1, 0):
             d_codes[l] = sb("d_codes%d" % l, [P, H], U32)
             nc.vector.tensor_copy(
                 d_codes[l][:].rearrange("p (t m) -> p m t", t=PACK),
-                picked[:].rearrange("p (m t) -> p m t", t=PACK),
+                picked[l][:].rearrange("p (m t) -> p m t", t=PACK),
             )
+        d_dealt = sb("d_dealt", [P, H], U8)
+        nc.vector.tensor_copy(
+            d_dealt[:].rearrange("p (t m) -> p m t", t=PACK),
+            d_moved[:].rearrange("p (m t) -> p m t", t=PACK),
+        )
         bias_t = sb("bias_t", [P, PACK], F32)
         nc.vector.scalar_tensor_tensor(bias_t[:], sl_t[:], -1.0, th_t[:], ALU.mult, ALU.mult)
 
         h = [sb("h%d" % t, [P, 2 * S], F32) for t in range(PACK)]
         st = [sb("st%d" % t, [P, 2 * S], F32) for t in range(PACK)]
-        for t in range(PACK):
-            nc.gpsimd.memset(h[t][:, S : 2 * S], 0.0)
-            nc.gpsimd.memset(st[t][:, S : 2 * S], 0.0)
-        larger = sb("larger", [P, PACK, S], F32)
-        for t in range(WHOLE):
+        larger = sb("larger", [P, PACK, S], F32, tag="d_moved")
+        for t in range(EARLY):
             nc.vector.tensor_tensor(larger[:, t, :], dt[t][:, 0:S], partner[t][:], ALU.max)
         z = sb("z", [P, S, PACK], BF16)
 
@@ -189,32 +190,37 @@ def tile_picked_cmixhaarhehq_none_p_kernel(
         weigh(0, slice(0, S))
         for c in range(2):
             cols = slice(HALF * c, HALF * (c + 1))
-            acc_h = [psum.tile([P, HALF], F32, name="acc_h%d_%d" % (c, t), tag="bank%d" % (4 * (1 - c) + t)) for t in range(PACK)]
+            acc_h = [
+                psum.tile([P, HALF], F32, name="acc_h%d_%d" % (c, t), tag="bank%d" % (PACK * (1 - c) + t))
+                for t in range(PACK)
+            ]
             for t in range(PACK):
                 rows = slice(P * t, P * (t + 1))
                 nc.tensor.matmul_mx(
                     out=acc_h[t][:],
                     lhsT=d_codes[1][:, rows].bitcast(FP8X4),
-                    lhsT_scale=d_planes[:, 1, rows],
+                    lhsT_scale=d_dealt[4:P, rows],
                     rhs=x2_words[:, cols].bitcast(FP8X4),
                     rhs_scale=x2_bytes[:, cols],
                     start=True,
                     stop=False,
                 )
-            for t in range(WHOLE, PACK):
+            for t in range(EARLY, PACK):
                 nc.vector.tensor_tensor(larger[:, t, cols], dt[t][:, cols], partner[t][:, cols], ALU.max)
-            weigh(2, cols)
+            weigh(EARLY, cols)
             z_codes = sb("z_codes%d" % c, [P, HALF], U32)
-            z_plane = sb("z_plane%d" % c, [P, HALF], U8)
-            nc.vector.quantize_mx(out=z_codes[:].bitcast(FP8X4), scales=z_plane[:], in_=z[:, cols, :].rearrange("p j t -> p (j t)"))
+            z_scales = sb("z_scales%d" % c, [P, HALF], U8)
+            nc.vector.quantize_mx(
+                out=z_codes[:].bitcast(FP8X4), scales=z_scales[:], in_=z[:, cols, :].rearrange("p j t -> p (j t)")
+            )
             for t in range(PACK):
                 rows = slice(P * t, P * (t + 1))
                 nc.tensor.matmul_mx(
                     out=acc_h[t][:],
                     lhsT=d_codes[0][:, rows].bitcast(FP8X4),
-                    lhsT_scale=d_planes[:, 0, rows],
+                    lhsT_scale=d_dealt[:, rows],
                     rhs=z_codes[:].bitcast(FP8X4),
-                    rhs_scale=z_plane[:],
+                    rhs_scale=z_scales[:],
                     start=False,
                     stop=True,
                 )
@@ -231,12 +237,13 @@ def tile_picked_cmixhaarhehq_none_p_kernel(
         for t in range(PACK):
             sg = sb("sg%d" % t, [P, S], F32)
             res = sb("res%d" % t, [P, S], F32)
-            nc.scalar.activation(
-                sg[:],
-                st[t][:].indirect(n5_t[:]),
-                ACT.Sigmoid,
-                bias=bias_t[:, t : t + 1],
-                scale=sl_t[:, t : t + 1],
-            )
-            nc.vector.tensor_tensor(res[:], h[t][:, 0:S], sg[:], ALU.mult)
-            nc.sync.dma_start(out_rows[:, t, :], res[:])
+            for cols in [slice(0, S)] if t < PACK - 1 else [slice(0, HALF), slice(HALF, S)]:
+                nc.scalar.activation(
+                    sg[:, cols],
+                    st[t][:].indirect(entries(n5_t, cols)),
+                    ACT.Sigmoid,
+                    bias=bias_t[:, t : t + 1],
+                    scale=sl_t[:, t : t + 1],
+                )
+                nc.vector.tensor_tensor(res[:, cols], h[t][:, cols], sg[:, cols], ALU.mult)
+                nc.sync.dma_start(out_rows[:, t, cols], res[:, cols])

from contextlib import ExitStack

import concourse.mybir as mybir

F32 = mybir.dt.float32
BF16 = mybir.dt.bfloat16
I32 = mybir.dt.int32
U32 = mybir.dt.uint32
U16 = mybir.dt.uint16
U8 = mybir.dt.uint8
FP8X4 = mybir.dt.float8_e4m3fn_x4
ALU = mybir.AluOpType
ACT = mybir.ActivationFunctionType

K, T, S, H, W, G = 512, 1024, 256, 512, 128, 2048
P = 128
PACK = 4
HALF = S // 2
SPARE = 8
EARLY = 2
W_SPLIT = 80
FLOPS = 3 * 2 * K * H * S


def tile_picked_cmixhaarhehq_none_p_kernel(
    tc, x_words, x_scales, w1, gs, d_words, d_scales, sl, th, offs, n1, n2, n3, k1, k2, two, n4, n5, out
):
    nc = tc.nc
    with ExitStack() as ctx:
        keep = ctx.enter_context(tc.tile_pool(name="keep", bufs=1))
        psum = ctx.enter_context(tc.psum_pool(name="psum", bufs=1))

        def sb(name, shape, dtype, tag=""):
            return keep.tile(shape, dtype, name=name, tag=tag or name, align_bytes=64)

        def load_list(name, src):
            tile = sb(name, list(src.shape), U16)
            nc.sync.dma_start(tile[:], src)
            return tile

        def entries(lists, cols):
            return lists[:, cols.start // 16 : cols.stop // 16]

        x_byte_table = sb("x_byte_table", [P, T], U8)
        d_byte_table = sb("d_byte_table", [P, G], U8)
        d_moved = sb("d_moved", [P, H], U8)
        nc.vector.memset(x_byte_table[:].bitcast(I32), 0)
        nc.vector.memset(d_byte_table[:].bitcast(I32), 0)
        nc.vector.memset(d_moved[:].bitcast(I32), 0)

        warm_in = sb("warm_in", [P, 1], F32)
        warm_out = sb("warm_out", [P, 1], F32)
        nc.vector.memset(warm_in[:], 0.0)
        nc.scalar.activation(warm_out[:], warm_in[:], ACT.Sigmoid)

        w_rows = w1.rearrange("(p j) c -> p j c", j=PACK)
        w_raw = sb("w_raw", [P, PACK, H], F32)
        nc.sync.dma_start(w_raw[:, 0:2, :], w_rows[:, 0:2, :])
        for r in range(4):
            nc.sync.dma_start(x_byte_table[r:P:32, :].bitcast(I32), x_scales[0, r:16:4, :].bitcast(I32))
        offs_t = load_list("offs_t", offs)
        nc.sync.dma_start(w_raw[:, 2:4, :], w_rows[:, 2:4, :])
        x_word_table = sb("x_word_table", [P, T], U32)
        nc.sync.dma_start(x_word_table[:].bitcast(I32), x_words[0].rearrange("p n t -> p (n t)").bitcast(I32))
        n1_t = load_list("n1_t", n1)
        n2_t = load_list("n2_t", n2)
        two_t = load_list("two_t", two)
        k1_t = load_list("k1_t", k1)
        nc.sync.dma_start(d_byte_table[0:P:8, :].bitcast(I32), d_scales[0].bitcast(I32))
        k2_t = load_list("k2_t", k2)
        d_word_table = sb("d_word_table", [P, G], U32)
        nc.sync.dma_start(d_word_table[:].bitcast(I32), d_words[0].rearrange("p n t -> p (n t)").bitcast(I32))
        n3_t = load_list("n3_t", n3)
        n4_t = load_list("n4_t", n4)
        n5_t = load_list("n5_t", n5)

        gs_t = sb("gs_t", [P, PACK], F32)
        sl_t = sb("sl_t", [P, PACK], F32)
        th_t = sb("th_t", [P, PACK], F32)
        for tile, src in ((gs_t, gs), (sl_t, sl), (th_t, th)):
            nc.sync.dma_start(tile[:], src.rearrange("(p t) o -> p (t o)", t=PACK))

        w_pairs = [sb("w_pairs%d" % u, [P, 2, P, PACK], BF16) for u in range(2)]
        xq_bytes = sb("xq_bytes", [P, S], U8)
        nc.vector.tensor_copy(xq_bytes[:], x_byte_table[:].indirect(offs_t[:]))
        w_src = w_raw[:].rearrange("p j (m t) -> p m j t", t=PACK)
        w_dst = [w_pairs[u][:].rearrange("p t m j -> p m j t") for u in range(2)]
        nc.vector.tensor_copy(w_dst[0][:, 0:W_SPLIT], w_src[:, 0:W_SPLIT, :, 0:2])
        nc.scalar.copy(w_dst[0][:, W_SPLIT:P], w_src[:, W_SPLIT:P, :, 0:2])
        nc.scalar.copy(w_dst[1], w_src[:, :, :, 2:4])
        w_codes = [sb("w_codes%d" % t, [P, P], U32) for t in range(PACK)]
        w_scales = [sb("w_scales%d" % t, [P, P], U8) for t in range(PACK)]

        def quantise_w(t):
            nc.vector.quantize_mx(
                out=w_codes[t][:].bitcast(FP8X4),
                scales=w_scales[t][:],
                in_=w_pairs[t // 2][:, t % 2, :, :].rearrange("p m j -> p (m j)"),
            )

        quantise_w(0)
        xq_words = sb("xq_words", [P, S], U32)
        nc.vector.tensor_copy(xq_words[:], x_word_table[:].indirect(offs_t[:]))
        for t in range(1, PACK):
            quantise_w(t)

        y = [sb("y%d" % t, [P, S], F32) for t in range(PACK)]
        pa = [sb("pa%d" % u, [P, 2, W], F32) for u in range(2)]
        pb = [sb("pb%d" % u, [P, 2, W], F32) for u in range(2)]
        ra = [sb("ra%d" % u, [P, 2, W], F32) for u in range(2)]
        rb = [sb("rb%d" % u, [P, 2, W], F32) for u in range(2)]
        dt = [sb("dt%d" % t, [P, S + SPARE], F32) for t in range(PACK)]
        partner = [sb("partner%d" % t, [P, S], F32) for t in range(PACK)]
        for t in range(PACK):
            acc_y = psum.tile([P, S], F32, name="acc_y%d" % t, tag="bank%d" % t)
            nc.tensor.matmul_mx(
                out=acc_y[:],
                lhsT=w_codes[t][:].bitcast(FP8X4),
                lhsT_scale=w_scales[t][:],
                rhs=xq_words[:].bitcast(FP8X4),
                rhs_scale=xq_bytes[:],
                start=True,
                stop=True,
            )
            if t == 0:
                nc.scalar.copy(y[t][:], acc_y[:])
            else:
                nc.vector.tensor_copy(y[t][:], acc_y[:])
        for t in range(PACK):
            nc.scalar.activation(pa[t // 2][:, t % 2, :], y[t][:].indirect(n1_t[:]), ACT.Copy)
            nc.scalar.activation(pb[t // 2][:, t % 2, :], y[t][:].indirect(n2_t[:]), ACT.Copy)
            if t % 2 == 1:
                nc.vector.tensor_tensor(ra[t // 2][:], pa[t // 2][:], pb[t // 2][:], ALU.add)
                nc.vector.tensor_tensor(rb[t // 2][:], pa[t // 2][:], pb[t // 2][:], ALU.subtract)
        for u in range(2):
            for lists, values in ((n1_t, ra[u]), (n2_t, rb[u])):
                for e in range(2):
                    nc.scalar.activation(dt[2 * u + e][:].indirect(lists[:]), values[:, e, :], ACT.Copy)
            for t in (2 * u, 2 * u + 1):
                cols = slice(0, S if t < EARLY else HALF)
                nc.scalar.activation(partner[t][:, cols], dt[t][:].indirect(entries(n3_t, cols)), ACT.Copy)
        for t in range(EARLY, PACK):
            cols = slice(HALF, S)
            nc.scalar.activation(partner[t][:, cols], dt[t][:].indirect(entries(n3_t, cols)), ACT.Copy)

        for l, lists in enumerate((k1_t, k2_t)):
            d_bytes = sb("d_bytes%d" % l, [P, H], U8, tag="w_codes%d" % (PACK - 1 - l))
            nc.vector.tensor_copy(d_bytes[:], d_byte_table[:].indirect(lists[:]))
            for r in range(4):
                nc.sync.dma_start(d_moved[4 * l + r : P : 32, :].bitcast(I32), d_bytes[8 * r : P : 32, :].bitcast(I32))
        x2_bytes = sb("x2_bytes", [P, S], U8, tag="w_scales%d" % (PACK - 1))
        nc.vector.tensor_copy(x2_bytes[:], x_byte_table[:].indirect(two_t[:]))
        x2_words = sb("x2_words", [P, S], U32)
        nc.vector.tensor_copy(x2_words[:], x_word_table[:].indirect(two_t[:]))
        picked = [None, None]
        for l, lists in ((1, k2_t), (0, k1_t)):
            picked[l] = sb("d_picked%d" % l, [P, H], U32, tag=("pa0", "pb0")[l])
            nc.vector.tensor_copy(picked[l][:], d_word_table[:].indirect(lists[:]))
        d_codes = [None, None]
        for l in (1, 0):
            d_codes[l] = sb("d_codes%d" % l, [P, H], U32)
            nc.vector.tensor_copy(
                d_codes[l][:].rearrange("p (t m) -> p m t", t=PACK),
                picked[l][:].rearrange("p (m t) -> p m t", t=PACK),
            )
        d_dealt = sb("d_dealt", [P, H], U8)
        nc.vector.tensor_copy(
            d_dealt[:].rearrange("p (t m) -> p m t", t=PACK),
            d_moved[:].rearrange("p (m t) -> p m t", t=PACK),
        )
        bias_t = sb("bias_t", [P, PACK], F32)
        nc.vector.scalar_tensor_tensor(bias_t[:], sl_t[:], -1.0, th_t[:], ALU.mult, ALU.mult)

        h = [sb("h%d" % t, [P, 2 * S], F32) for t in range(PACK)]
        st = [sb("st%d" % t, [P, 2 * S], F32) for t in range(PACK)]
        larger = sb("larger", [P, PACK, S], F32, tag="d_moved")
        for t in range(EARLY):
            nc.vector.tensor_tensor(larger[:, t, :], dt[t][:, 0:S], partner[t][:], ALU.max)
        z = sb("z", [P, S, PACK], BF16)

        def weigh(t0, cols):
            groups = (cols.stop - cols.start) // 4
            nc.vector.tensor_tensor(
                z[:, cols, t0 : t0 + 2].rearrange("p (c i) t -> p c t i", i=4),
                larger[:, t0 : t0 + 2, cols].rearrange("p t (c i) -> p c t i", i=4),
                gs_t[:, t0 : t0 + 2].unsqueeze(1).unsqueeze(3).to_broadcast([P, groups, 2, 4]),
                ALU.mult,
            )

        weigh(0, slice(0, S))
        for c in range(2):
            cols = slice(HALF * c, HALF * (c + 1))
            acc_h = [
                psum.tile([P, HALF], F32, name="acc_h%d_%d" % (c, t), tag="bank%d" % (PACK * (1 - c) + t))
                for t in range(PACK)
            ]
            for t in range(PACK):
                rows = slice(P * t, P * (t + 1))
                nc.tensor.matmul_mx(
                    out=acc_h[t][:],
                    lhsT=d_codes[1][:, rows].bitcast(FP8X4),
                    lhsT_scale=d_dealt[4:P, rows],
                    rhs=x2_words[:, cols].bitcast(FP8X4),
                    rhs_scale=x2_bytes[:, cols],
                    start=True,
                    stop=False,
                )
            for t in range(EARLY, PACK):
                nc.vector.tensor_tensor(larger[:, t, cols], dt[t][:, cols], partner[t][:, cols], ALU.max)
            weigh(EARLY, cols)
            z_codes = sb("z_codes%d" % c, [P, HALF], U32)
            z_scales = sb("z_scales%d" % c, [P, HALF], U8)
            nc.vector.quantize_mx(
                out=z_codes[:].bitcast(FP8X4), scales=z_scales[:], in_=z[:, cols, :].rearrange("p j t -> p (j t)")
            )
            for t in range(PACK):
                rows = slice(P * t, P * (t + 1))
                nc.tensor.matmul_mx(
                    out=acc_h[t][:],
                    lhsT=d_codes[0][:, rows].bitcast(FP8X4),
                    lhsT_scale=d_dealt[:, rows],
                    rhs=z_codes[:].bitcast(FP8X4),
                    rhs_scale=z_scales[:],
                    start=False,
                    stop=True,
                )
                if c == 0:
                    nc.scalar.activation(h[t][:, cols], acc_h[t][:], ACT.Copy, scale=0.0625)
                else:
                    nc.vector.tensor_scalar(h[t][:, cols], acc_h[t][:], 0.0625, None, ALU.mult)

        out_rows = out.rearrange("(p t) j -> p t j", t=PACK)
        for t in range(PACK):
            other = sb("other%d" % t, [P, S], F32)
            nc.scalar.activation(other[:], h[t][:].indirect(n4_t[:]), ACT.Copy)
            nc.vector.tensor_tensor(st[t][:, 0:S], h[t][:, 0:S], other[:], ALU.subtract)
        for t in range(PACK):
            sg = sb("sg%d" % t, [P, S], F32)
            res = sb("res%d" % t, [P, S], F32)
            for cols in [slice(0, S)] if t < PACK - 1 else [slice(0, HALF), slice(HALF, S)]:
                nc.scalar.activation(
                    sg[:, cols],
                    st[t][:].indirect(entries(n5_t, cols)),
                    ACT.Sigmoid,
                    bias=bias_t[:, t : t + 1],
                    scale=sl_t[:, t : t + 1],
                )
                nc.vector.tensor_tensor(res[:, cols], h[t][:, cols], sg[:, cols], ALU.mult)
                nc.sync.dma_start(out_rows[:, t, cols], res[:, cols])
